import numpy as np
CORES = [5,13,29,37,53,69,77,101,133,141,157,165,181,197,205,229]
N = 16
V, DEP = 16384, 4
def entries(a): return a.T.reshape(-1)
def pack(v, P): return np.ascontiguousarray(np.asarray(v, np.int32).reshape(-1, P).T)
def forest(rng, n, lev):
    P = np.arange(n)
    for l in range(1, int(lev.max()) + 1):
        a, b = np.nonzero(lev == l)[0], np.nonzero(lev == l - 1)[0]; P[a] = b[rng.integers(0, len(b), len(a))]
    return P
def lists(rng, how):
    n = N * V; P = np.arange(n)
    if how == "uniform":
        lev = rng.integers(0, DEP + 1, n); lev[rng.permutation(n)[:DEP + 1]] = np.arange(DEP + 1); P = forest(rng, n, lev)
    if how == "star":
        lev = np.ones(n, np.int64); lev[rng.permutation(n)[:4]] = 0; P = forest(rng, n, lev)
    if how == "chain":
        W = np.stack([V * r + rng.permutation(V)[:V // (DEP + 1) * (DEP + 1)].reshape(-1, DEP + 1) for r in range(N)]); P[W[:, :, 1:]] = np.roll(W, 1, axis=0)[:, :, :-1]
    if how == "deep":
        z = rng.permutation(N); g = V * z[1 + np.arange(DEP) % (N - 1)] + rng.permutation(V)[:DEP]; P[:] = g[-1]; P[g] = np.concatenate([g[:1], g[:-1]])
    if how == "whole":
        o = rng.permutation(N)
        for i in range(1, N - 1):
            if i % (DEP + 1): P[V * o[i]:V * o[i] + V] = V * o[i - 1] + rng.permutation(V)
        P[V * o[-1]:V * o[-1] + V] = V * o[-1] + forest(rng, V, rng.permutation(np.concatenate([np.arange(DEP + 1), rng.integers(0, DEP + 1, V - DEP - 1)])))
    return {"par": np.stack([pack(p, 16) for p in P.reshape(N, V)])}
def setup_inputs(rng):
    return dict({"val": rng.standard_normal((N, 16, V // 16), dtype=np.float32)}, **lists(rng, "uniform"))
def setup_inputs_chain(rng):
    d = setup_inputs(rng); d.update(lists(rng, "chain"))
    for k in ("val",): d[k] = (d[k].astype(np.float32) * 1048576.0).astype(d[k].dtype)
    return d
def setup_inputs_deep(rng):
    d = setup_inputs(rng); d.update(lists(rng, "deep"))
    for k in ("val",): d[k] = (d[k].astype(np.float32) * (1 / 1024.0)).astype(d[k].dtype)
    return d
def setup_inputs_star(rng):
    d = setup_inputs(rng); d.update(lists(rng, "star"))
    return d
def setup_inputs_whole(rng):
    d = setup_inputs(rng); d.update(lists(rng, "whole"))
    return d
def check_inputs(x):
    bad = []
    if x["par"].min() < 0 or x["par"].max() >= N * V: bad.append("par out of range")
    p = np.concatenate([entries(a) for a in x["par"]]); q = p
    for k in range(DEP - 1): q = p[q]
    if (p[q] != q).any(): bad.append("a node is more than DEP hops from a root")
    return bad
def reference(val, par):
    p = np.concatenate([entries(a) for a in par]); v = np.concatenate([entries(a) for a in val])
    q = p
    for k in range(DEP - 1): q = p[q]
    return {"y": np.stack([np.ascontiguousarray(v[q][V * r:V * r + V].reshape(-1, 16).T) for r in range(N)])}

@@ -1,0 +1,319 @@
+from concourse.bass import DstId, RemoteDMATransfer
+from concourse.mybir import AluOpType as Op, ActivationFunctionType as Act
+
+N, HOPS, WORLD = 16, 4, 256
+ONE = 262144.0
+WIN = 2056
+SCRATCH = {
+    "fp": ("dram", [16, 128, 128], "int32"), "fv": ("dram", [16, 128, 128], "float32"),
+    "tabp": ("sbuf", [128, WIN], "int32"), "tabv": ("sbuf", [128, WIN], "float32"),
+    "own": ("sbuf", [128, 128], "int32"), "q0": ("sbuf", [128, 8], "int32"),
+    "ri": ("sbuf", [128, 128], "int32"), "rj": ("sbuf", [128, 128], "int32"),
+    "mx": ("sbuf", [128, 64], "float32"), "offs": ("sbuf", [128, 64], "uint16"),
+    "gm": ("sbuf", [128, 1024], "float32"), "stt": ("sbuf", [128, 8, 32], "float32"),
+    "stp": ("sbuf", [128, 8, 32], "float32"), "mk": ("sbuf", [128, 8, 18], "float32"),
+    "zz": ("sbuf", [128, 128], "float32"), "zs": ("sbuf", [128, 128], "float32"), "keep": ("sbuf", [128, 64], "float32"),
+    "ysb": ("sbuf", [128, 8], "float32"), "ybuf": ("sbuf", [128, 128], "float32"),
+    "cmod": ("sbuf", [128, 128], "float32"), "cs": ("sbuf", [128, 32], "float32"), "mhc": ("sbuf", [128, 32], "float32"),
+    "labs": ("sbuf", [128, 64], "float32"), "pidx": ("sbuf", [128, 1], "int32"), "pint": ("sbuf", [128, 2], "int32"),
+    "pflt": ("sbuf", [128, 2], "float32"), "bias": ("sbuf", [128, 1], "float32"),
+    "spread": ("sbuf", [128, 128], "float32"), "mmh": ("sbuf", [128, 32], "float32"),
+    "selp": ("sbuf", [128, 32], "float32"), "selv": ("sbuf", [128, 16], "float32"),
+    "cv0": ("psum", [128, 512], "float32"), "cv1": ("psum", [128, 512], "float32"),
+    "li0": ("psum", [128, 512], "float32"), "li1": ("psum", [128, 512], "float32"), "lab": ("psum", [128, 512], "float32"),
+}
+SEMAPHORES = (["ldp", "ldv", "tpl", "tvl", "q0s", "q0r", "snd", "ya", "ys", "yd", "raw", "vc", "vn"]
+              + ["ap%d" % r for r in range(N)] + ["av%d" % r for r in range(N)]
+              + ["%s%d" % (s, k) for s in ("sc", "mx", "ri", "rj", "mk", "st", "of", "cs", "pl", "zz", "zs") for k in (0, 1)]
+              + ["gc%d" % k for k in range(8)])
+PLAN = {}
+
+
+def bits(m):
+    return bin(m).count("1")
+
+
+def plan(T, topo):
+    if PLAN:
+        return PLAN
+    chips = {}
+    for c in range(WORLD):
+        chips.setdefault((topo.host(c), topo.chip(c)), []).append(c)
+    crews = list(chips.values())
+    crew_of = {c: k for k in crews for c in k}
+    cross = {c: [] for c in range(WORLD)}
+    came = {c: 0 for c in range(WORLD)}
+    enters = {}
+    for r in range(N):
+        home = T.cores[r]
+        crew = crew_of[home]
+        owners = [c for c in crew if all(topo.may_write(c, k[0]) for k in crews if k is not crew)]
+        plain = [home] + [c for c in crew if c not in owners and c != home]
+        at = crews.index(crew)
+        for s in range(1, len(crews)):
+            k = crews[(at + s) % len(crews)]
+            who = min(plain if topo.same_plane(home, k[0]) else owners,
+                      key=lambda c: (len(cross[c]), enters.get((k[0], topo.die(c)), 0)))
+            cross[who].append(k)
+            enters[(k[0], topo.die(who))] = enters.get((k[0], topo.die(who)), 0) + 1
+            came[k[r // 2]] = bits(topo.mask(who, k[r // 2]))
+    job, left = {}, []
+    for r in range(N):
+        for k, c in enumerate(crew_of[T.cores[r]]):
+            job[c] = (r, k)
+        left += [(r, k) for k in range(8, 16)]
+    spare = [c for c in range(WORLD) if c not in job]
+    spare.sort(key=lambda c: (sum(topo.may_write(c, d) for d in T.cores), c))
+    asked = {}
+    asks = {c: [] for c in range(WORLD)}
+    for c in spare:
+        r, k = min([x for x in left if topo.may_write(c, T.cores[x[0]])],
+                   key=lambda x: (-sum(y[0] == x[0] for y in left), x))
+        left.remove((r, k))
+        job[c] = (r, k)
+        who = min([d for d in crew_of[T.cores[r]] if topo.may_write(d, c)], key=lambda d: (len(asks[d]), len(cross[d])))
+        asks[who].append((c, k))
+        asked[c] = bits(topo.mask(who, c))
+    PLAN.update(crew_of=crew_of, cross=cross, came=came, job=job, asks=asks, asked=asked)
+    return PLAN
+
+
+def rank_program(g, core, T, topo):
+    pl = plan(T, topo)
+    crew = pl["crew_of"][core]
+    me = crew.index(core)
+    others = [c for c in crew if c != core]
+    rank = ([r for r in range(N) if T.cores[r] in crew] + [-1])[0]
+    job, piece = pl["job"][core]
+    home = T.cores[job]
+    sent = [0]
+
+    def send(src, dsts, sem):
+        m = 0xFFFF
+        for c, p in dsts:
+            m &= topo.mask(core, c)
+        ids = []
+        for c, p in dsts:
+            rid, pid = topo.addr(c, core)
+            ids.append(DstId(rid=rid, pnc=pid))
+        g.remote_dma_fused([RemoteDMATransfer(dst_ids=ids, dma_engine_mask=m, remote_sem=sem, srcs=[src],
+                                              dsts=[p for c, p in dsts])], local_sem=T.sem.snd)
+        sent[0] += bits(m)
+    on_chip = bits(topo.mask(core, others[0]))
+    slots = [r for r in (2 * me, 2 * me + 1) if r != rank]
+
+    def here(q, r, what):
+        if r == rank and core == home:
+            q.wait_ge(T.sem["ld" + what], 16)
+        else:
+            q.wait_ge(T.sem["a%s%d" % (what, r)], pl["came"][core] if r in slots else on_chip)
+
+    y, s = g.sync, g.scalar
+    if core == home:
+        y.dma_start(T.fp[rank], T.par[:]).then_inc(T.sem.ldp, 16)
+        s.dma_start(T.own[:], T.par[:]).then_inc(T.sem.q0s, 16)
+        s.dma_start(T.fv[rank], T.val[:]).then_inc(T.sem.ldv, 16)
+    elif rank >= 0:
+        here(y, rank, "p")
+        y.dma_start(T.own[:], T.fp[rank]).then_inc(T.sem.q0s, 16)
+    order = sorted(range(N), key=lambda r: (r != rank, r not in slots, r % 2, (r // 2 - me) % 8))
+    y.wait_ge(T.sem.vc, 4)
+    s.wait_ge(T.sem.vc, 4)
+    for tab, full, what, done in ((T.tabp, T.fp, "p", T.sem.tpl), (T.tabv, T.fv, "v", T.sem.tvl)):
+        for i, r in enumerate(order):
+            q = s if what == "p" and i % 2 else y
+            here(q, r, what)
+            a, b = 16 * (r // 2), 4 + 1024 * (r % 2)
+            q.dma_start(tab[a:a + 16, b:b + 1024], full[r]).then_inc(done, 16)
+
+    g.iota(T.pidx[:], [[0, 1]], 0, 1).then_inc(T.sem.raw, 1)
+    for buf, pattern in ((T.cmod, [[0, 8], [1, 16]]), (T.cs, [[1, 32]]), (T.mhc, [[0, 4], [1, 8]]), (T.labs, [[0, 4], [1, 16]])):
+        g.iota(buf[:], pattern, 0, 0, allow_small_or_imprecise_dtypes=True).then_inc(T.sem.raw, 1)
+
+    def share(full, what):
+        if core == home:
+            here(g, rank, what)
+            send(full[rank], [(c, full[rank]) for c in others], T.sem["a%s%d" % (what, rank)])
+
+    def crossing(full, what):
+        if pl["cross"][core]:
+            here(g, rank, what)
+            send(full[rank], [(k[rank // 2], full[rank]) for k in pl["cross"][core]], T.sem["a%s%d" % (what, rank)])
+
+    def broadcast(full, what):
+        for r in slots:
+            here(g, r, what)
+            send(full[r], [(c, full[r]) for c in others], T.sem["a%s%d" % (what, r)])
+    share(T.fp, "p")
+    crossing(T.fp, "p")
+    if pl["asks"][core]:
+        g.wait_ge(T.sem.q0s, 16)
+        for c, k in pl["asks"][core]:
+            send(T.own[:, 8 * k:8 * k + 8], [(c, T.q0[:])], T.sem.q0r)
+    share(T.fv, "v")
+    broadcast(T.fp, "p")
+    crossing(T.fv, "v")
+    broadcast(T.fv, "v")
+
+    v, t = g.vector, g.tensor
+    vc = [0]
+
+    def con(ins):
+        ins.then_inc(T.sem.vc, 1)
+        vc[0] += 1
+    for tab in (T.tabp, T.tabv):
+        con(v.memset(tab[:, 0:4], 0))
+        con(v.memset(tab[:, WIN - 4:WIN], 0))
+    v.wait_ge(T.sem.vc, 4)
+    v.wait_ge(T.sem.raw, 5)
+    v.sem_inc(T.sem.vn, 1)
+    n = [0]
+
+    def con2(ins):
+        ins.then_inc(T.sem.vn, 1)
+        n[0] += 1
+    n[0] = 1
+    con2(v.tensor_scalar(T.pint[:, 0:1], T.pidx[:], 15, None, Op.bitwise_and))
+    con2(v.tensor_scalar(T.pint[:, 1:2], T.pidx[:], 4, None, Op.arith_shift_right))
+    con2(v.memset(T.stp[:], 0.0))
+    con2(v.memset(T.mk[:], 0.0))
+    con2(v.memset(T.keep[:], 1.0))
+    v.wait_ge(T.sem.vn, n[0])
+    con2(v.tensor_copy(T.pflt[:], T.pint[:]))
+    con2(v.memset(T.keep[:, ::16], 0.0))
+    con2(v.tensor_copy(T.lab[:, 0:64], T.labs[:]))
+    v.wait_ge(T.sem.vn, n[0])
+    con2(v.tensor_scalar(T.spread[:], T.cmod[:], T.pflt[:, 0:1], ONE / 16, Op.is_equal, Op.mult))
+    con2(v.tensor_scalar(T.selp[:], T.cs[:], T.pflt[:, 0:1], 1.0 / ONE, Op.is_equal, Op.mult))
+    con2(v.tensor_scalar(T.selv[:], T.cs[:, 0:16], T.pflt[:, 0:1], None, Op.is_equal))
+    con2(v.tensor_scalar(T.mmh[:], T.mhc[:], T.pflt[:, 1:2], None, Op.is_equal))
+    con2(v.tensor_scalar(T.bias[:], T.pflt[:, 1:2], -2048.0, 4.0 - 0.46875 - ONE / 16, Op.mult, Op.add))
+    v.wait_ge(T.sem.vn, n[0])
+    consts = n[0]
+    if rank >= 0:
+        v.wait_ge(T.sem.q0s, 16)
+    else:
+        v.wait_ge(T.sem.q0r, pl["asked"][core])
+    for k in range(16, 32):
+        con2(v.tensor_scalar(T.stt[:, :, k], T.own[:, 8 * piece:8 * piece + 8] if rank >= 0 else T.q0[:], 1.0 / ONE, 1.0,
+                             Op.mult, Op.add))
+    v.wait_ge(T.sem.vn, n[0])
+
+    def masked(p, h):
+        v.tensor_tensor(T.mx[:, 32 * p:32 * p + 32], T.stt[:, 4 * p:4 * p + 4, 16:24], T.mmh[:], Op.mult).then_inc(
+            T.sem["mx%d" % p], 1)
+
+    def low(p, h):
+        a, b = 64 * p, 64 * p + 64
+        v.tensor_scalar(T.ri[:, a:b], T.stt[:, 4 * p:4 * p + 4, 16:32], ONE, -ONE, Op.mult, Op.add).then_inc(T.sem["ri%d" % p], 1)
+        v.wait_ge(T.sem["ri%d" % p], h)
+        v.tensor_scalar(T.rj[:, a:b], T.ri[:, a:b], 15, None, Op.bitwise_and).then_inc(T.sem["rj%d" % p], 1)
+
+    def choice(p, h):
+        i, j = 4 * p, 4 * p + 4
+        v.wait_ge(T.sem["rj%d" % p], h)
+        v.tensor_tensor(T.mk[:, i:j, 1:17], T.rj[:, 64 * p:64 * p + 64], T.lab[:, 0:64], Op.is_equal).then_inc(
+            T.sem["mk%d" % p], 1)
+        if h < HOPS:
+            v.wait_ge(T.sem["mk%d" % p], h)
+            v.tensor_tensor(T.stp[:, i:j, 0:17], T.mk[:, i:j, 0:17], T.mk[:, i:j, 1:18], Op.subtract).then_inc(
+                T.sem["st%d" % p], 1)
+
+    def columns(p, h):
+        v.wait_ge(T.sem["pl%d" % p], h)
+        v.tensor_scalar(T.offs[:, 32 * p:32 * p + 32], T["li%d" % p][:, 0:32], T.bias[:, 0:1], 2052.0, Op.add, Op.min).then_inc(
+            T.sem["of%d" % p], 1)
+
+    def window(h):
+        return (T.tabp if h < HOPS else T.tabv)[:, 0:WIN]
+
+    def gather(p, h):
+        v.wait_ge(T.sem["of%d" % p], h)
+        for k in (4 * p, 4 * p + 1):
+            v.tensor_copy(T.gm[:, 128 * k:128 * k + 128], window(h).indirect(T.offs[:, 8 * k:8 * k + 8])).then_inc(
+                T.sem["gc%d" % k], 1)
+
+    def pick(p, h):
+        v.wait_ge(T.sem["cs%d" % p], 4 * h)
+        v.wait_ge(T.sem["st%d" % p], h)
+        for k in range(4):
+            v.tensor_tensor_scan(T.stt[:, 4 * p + k, :], T.stp[:, 4 * p + k, :], T["cv%d" % p][:, 32 * k:32 * k + 32], 0.0,
+                                 Op.add, Op.max).then_inc(T.sem["sc%d" % p], 1)
+        v.wait_ge(T.sem["sc%d" % p], 4 * h)
+        masked(p, h + 1)
+        low(p, h + 1)
+
+    for p in (0, 1):
+        masked(p, 1)
+        low(p, 1)
+    for p in (0, 1):
+        columns(p, 1)
+        choice(p, 1)
+    for q in (v, s):
+        q.wait_ge(T.sem.tpl, 16 * N)
+    gather(0, 1)
+    for h in range(1, HOPS + 1):
+        if h > 1:
+            if h == HOPS:
+                v.wait_ge(T.sem.tvl, 16 * N)
+            gather(0, h)
+            choice(0, h)
+            pick(1, h - 1)
+            columns(1, h)
+        gather(1, h)
+        if h > 1:
+            choice(1, h)
+        if h < HOPS:
+            pick(0, h)
+            columns(0, h + 1)
+    out, base = (T.ybuf, 8 * piece) if core == home else (T.ysb, 0)
+    for p in (0, 1):
+        a, b = 64 * p, 64 * p + 64
+        v.wait_ge(T.sem["cs%d" % p], 4 * HOPS)
+        v.wait_ge(T.sem["mk%d" % p], HOPS)
+        v.tensor_tensor(T.zz[:, a:b], T["cv%d" % p][:, 0:64], T.mk[:, 4 * p:4 * p + 4, 1:17], Op.mult).then_inc(T.sem["zz%d" % p], 1)
+        v.wait_ge(T.sem["zz%d" % p], 1)
+        v.tensor_tensor_scan(T.zs[:, a:b], T.keep[:], T.zz[:, a:b], 0.0, Op.mult, Op.add).then_inc(T.sem["zs%d" % p], 1)
+        v.wait_ge(T.sem["zs%d" % p], 1)
+        v.tensor_copy(out[:, base + 4 * p:base + 4 * p + 4], T.zs[:, a + 15:b:16]).then_inc(T.sem.ys, 1)
+    for h in range(1, HOPS + 1):
+        if h == HOPS:
+            s.wait_ge(T.sem.tvl, 16 * N)
+        for p in (0, 1):
+            s.wait_ge(T.sem["of%d" % p], h)
+            for k in (4 * p + 2, 4 * p + 3):
+                s.activation(T.gm[:, 128 * k:128 * k + 128], window(h).indirect(T.offs[:, 8 * k:8 * k + 8]), Act.Copy).then_inc(
+                    T.sem["gc%d" % k], 1)
+
+    def lists(p, h):
+        t.wait_ge(T.sem["mx%d" % p], h)
+        t.matmul(T["li%d" % p][:, 0:32], T.spread[:], T.mx[:, 32 * p:32 * p + 32], True, True).then_inc(T.sem["pl%d" % p], 1)
+
+    def total(p, h, ks):
+        w, sel = (32, T.selp) if h < HOPS else (16, T.selv)
+        for k in ks:
+            t.wait_ge(T.sem["gc%d" % (4 * p + k)], h)
+            t.matmul(T["cv%d" % p][:, w * k:w * k + w], T.gm[:, 512 * p + 128 * k:512 * p + 128 * k + 128], sel[:],
+                     True, True).then_inc(T.sem["cs%d" % p], 1)
+    t.wait_ge(T.sem.vn, consts)
+    lists(0, 1)
+    lists(1, 1)
+    for h in range(1, HOPS + 1):
+        total(0, h, (0, 2))
+        if h > 1:
+            lists(1, h)
+        total(0, h, (1, 3))
+        total(1, h, (0, 2))
+        if h < HOPS:
+            lists(0, h + 1)
+        total(1, h, (1, 3))
+
+    if core != home:
+        g.wait_ge(T.sem.ys, 2)
+        send(T.ysb[:], [(home, T.ybuf[:, 8 * piece:8 * piece + 8])], T.sem.ya)
+    else:
+        y.wait_ge(T.sem.ys, 2)
+        y.wait_ge(T.sem.ya, sum(bits(topo.mask(c, core)) for c, x in pl["job"].items() if x[0] == job and c != core))
+        y.dma_start(T.y[:], T.ybuf[:]).then_inc(T.sem.yd, 16)
+        y.wait_ge(T.sem.yd, 16)
+    g.wait_ge(T.sem.snd, sent[0])

@@ -22,7 +22,7 @@ SCRATCH = {
     "cv0": ("psum", [128, 512], "float32"), "cv1": ("psum", [128, 512], "float32"),
     "li0": ("psum", [128, 512], "float32"), "li1": ("psum", [128, 512], "float32"), "lab": ("psum", [128, 512], "float32"),
 }
-SEMAPHORES = (["ldp", "ldv", "tpl", "tvl", "q0s", "q0r", "snd", "ya", "ys", "yd", "raw", "vc", "vn"]
+SEMAPHORES = (["ldp", "ldv", "tpl", "tvl", "q0s", "q0r", "snd", "ya", "ys", "yd", "raw", "vc", "vn", "vi"]
               + ["ap%d" % r for r in range(N)] + ["av%d" % r for r in range(N)]
               + ["%s%d" % (s, k) for s in ("sc", "mx", "ri", "rj", "mk", "st", "of", "cs", "pl", "zz", "zs") for k in (0, 1)]
               + ["gc%d" % k for k in range(8)])
@@ -114,17 +114,14 @@ def rank_program(g, core, T, topo):
         s.dma_start(T.own[:], T.par[:]).then_inc(T.sem.q0s, 16)
         s.dma_start(T.fv[rank], T.val[:]).then_inc(T.sem.ldv, 16)
     elif rank >= 0:
-        here(y, rank, "p")
-        y.dma_start(T.own[:], T.fp[rank]).then_inc(T.sem.q0s, 16)
-    order = sorted(range(N), key=lambda r: (r != rank, r not in slots, r % 2, (r // 2 - me) % 8))
+        here(s, rank, "p")
+        s.dma_start(T.own[:], T.fp[rank]).then_inc(T.sem.q0s, 16)
     y.wait_ge(T.sem.vc, 4)
-    s.wait_ge(T.sem.vc, 4)
     for tab, full, what, done in ((T.tabp, T.fp, "p", T.sem.tpl), (T.tabv, T.fv, "v", T.sem.tvl)):
-        for i, r in enumerate(order):
-            q = s if what == "p" and i % 2 else y
-            here(q, r, what)
-            a, b = 16 * (r // 2), 4 + 1024 * (r % 2)
-            q.dma_start(tab[a:a + 16, b:b + 1024], full[r]).then_inc(done, 16)
+        for odd in (0, 1):
+            for r in range(odd, N, 2):
+                here(y, r, what)
+            y.dma_start(tab[:, 4 + 1024 * odd:1028 + 1024 * odd], full[odd::2]).then_inc(done, 16)
 
     g.iota(T.pidx[:], [[0, 1]], 0, 1).then_inc(T.sem.raw, 1)
     for buf, pattern in ((T.cmod, [[0, 8], [1, 16]]), (T.cs, [[1, 32]]), (T.mhc, [[0, 4], [1, 8]]), (T.labs, [[0, 4], [1, 16]])):
@@ -156,48 +153,40 @@ def rank_program(g, core, T, topo):
     broadcast(T.fv, "v")
 
     v, t = g.vector, g.tensor
-    vc = [0]
-
-    def con(ins):
-        ins.then_inc(T.sem.vc, 1)
-        vc[0] += 1
     for tab in (T.tabp, T.tabv):
-        con(v.memset(tab[:, 0:4], 0))
-        con(v.memset(tab[:, WIN - 4:WIN], 0))
-    v.wait_ge(T.sem.vc, 4)
-    v.wait_ge(T.sem.raw, 5)
-    v.sem_inc(T.sem.vn, 1)
+        v.memset(tab[:, 0:4], 0).then_inc(T.sem.vc, 1)
+        v.memset(tab[:, WIN - 4:WIN], 0).then_inc(T.sem.vc, 1)
     n = [0]
 
-    def con2(ins):
+    def con(ins):
         ins.then_inc(T.sem.vn, 1)
         n[0] += 1
-    n[0] = 1
-    con2(v.tensor_scalar(T.pint[:, 0:1], T.pidx[:], 15, None, Op.bitwise_and))
-    con2(v.tensor_scalar(T.pint[:, 1:2], T.pidx[:], 4, None, Op.arith_shift_right))
-    con2(v.memset(T.stp[:], 0.0))
-    con2(v.memset(T.mk[:], 0.0))
-    con2(v.memset(T.keep[:], 1.0))
+    v.wait_ge(T.sem.raw, 5)
+    con(v.tensor_scalar(T.pint[:, 0:1], T.pidx[:], 15, None, Op.bitwise_and))
+    con(v.tensor_scalar(T.pint[:, 1:2], T.pidx[:], 4, None, Op.arith_shift_right))
+    con(v.memset(T.stp[:], 0.0))
+    con(v.memset(T.mk[:], 0.0))
+    con(v.memset(T.keep[:], 1.0))
     v.wait_ge(T.sem.vn, n[0])
-    con2(v.tensor_copy(T.pflt[:], T.pint[:]))
-    con2(v.memset(T.keep[:, ::16], 0.0))
-    con2(v.tensor_copy(T.lab[:, 0:64], T.labs[:]))
+    con(v.tensor_copy(T.pflt[:], T.pint[:]))
+    con(v.memset(T.keep[:, ::16], 0.0))
+    con(v.tensor_copy(T.lab[:, 0:64], T.labs[:]))
     v.wait_ge(T.sem.vn, n[0])
-    con2(v.tensor_scalar(T.spread[:], T.cmod[:], T.pflt[:, 0:1], ONE / 16, Op.is_equal, Op.mult))
-    con2(v.tensor_scalar(T.selp[:], T.cs[:], T.pflt[:, 0:1], 1.0 / ONE, Op.is_equal, Op.mult))
-    con2(v.tensor_scalar(T.selv[:], T.cs[:, 0:16], T.pflt[:, 0:1], None, Op.is_equal))
-    con2(v.tensor_scalar(T.mmh[:], T.mhc[:], T.pflt[:, 1:2], None, Op.is_equal))
-    con2(v.tensor_scalar(T.bias[:], T.pflt[:, 1:2], -2048.0, 4.0 - 0.46875 - ONE / 16, Op.mult, Op.add))
+    con(v.tensor_scalar(T.spread[:], T.cmod[:], T.pflt[:, 0:1], ONE / 16, Op.is_equal, Op.mult))
+    con(v.tensor_scalar(T.selp[:], T.cs[:], T.pflt[:, 0:1], 1.0 / ONE, Op.is_equal, Op.mult))
+    con(v.tensor_scalar(T.selv[:], T.cs[:, 0:16], T.pflt[:, 0:1], None, Op.is_equal))
+    con(v.tensor_scalar(T.mmh[:], T.mhc[:], T.pflt[:, 1:2], None, Op.is_equal))
+    con(v.tensor_scalar(T.bias[:], T.pflt[:, 1:2], -2048.0, 4.0 - 0.46875 - ONE / 16, Op.mult, Op.add))
+    v.wait_ge(T.sem.vc, 4)
     v.wait_ge(T.sem.vn, n[0])
-    consts = n[0]
     if rank >= 0:
         v.wait_ge(T.sem.q0s, 16)
     else:
         v.wait_ge(T.sem.q0r, pl["asked"][core])
     for k in range(16, 32):
-        con2(v.tensor_scalar(T.stt[:, :, k], T.own[:, 8 * piece:8 * piece + 8] if rank >= 0 else T.q0[:], 1.0 / ONE, 1.0,
-                             Op.mult, Op.add))
-    v.wait_ge(T.sem.vn, n[0])
+        v.tensor_scalar(T.stt[:, :, k], T.own[:, 8 * piece:8 * piece + 8] if rank >= 0 else T.q0[:], 1.0 / ONE, 1.0,
+                        Op.mult, Op.add).then_inc(T.sem.vi, 1)
+    v.wait_ge(T.sem.vi, 16)
 
     def masked(p, h):
         v.tensor_tensor(T.mx[:, 32 * p:32 * p + 32], T.stt[:, 4 * p:4 * p + 4, 16:24], T.mmh[:], Op.mult).then_inc(
@@ -250,12 +239,12 @@ def rank_program(g, core, T, topo):
         columns(p, 1)
         choice(p, 1)
     for q in (v, s):
-        q.wait_ge(T.sem.tpl, 16 * N)
+        q.wait_ge(T.sem.tpl, 32)
     gather(0, 1)
     for h in range(1, HOPS + 1):
         if h > 1:
             if h == HOPS:
-                v.wait_ge(T.sem.tvl, 16 * N)
+                v.wait_ge(T.sem.tvl, 32)
             gather(0, h)
             choice(0, h)
             pick(1, h - 1)
@@ -278,7 +267,7 @@ def rank_program(g, core, T, topo):
         v.tensor_copy(out[:, base + 4 * p:base + 4 * p + 4], T.zs[:, a + 15:b:16]).then_inc(T.sem.ys, 1)
     for h in range(1, HOPS + 1):
         if h == HOPS:
-            s.wait_ge(T.sem.tvl, 16 * N)
+            s.wait_ge(T.sem.tvl, 32)
         for p in (0, 1):
             s.wait_ge(T.sem["of%d" % p], h)
             for k in (4 * p + 2, 4 * p + 3):
@@ -295,7 +284,7 @@ def rank_program(g, core, T, topo):
             t.wait_ge(T.sem["gc%d" % (4 * p + k)], h)
             t.matmul(T["cv%d" % p][:, w * k:w * k + w], T.gm[:, 512 * p + 128 * k:512 * p + 128 * k + 128], sel[:],
                      True, True).then_inc(T.sem["cs%d" % p], 1)
-    t.wait_ge(T.sem.vn, consts)
+    t.wait_ge(T.sem.vn, n[0])
     lists(0, 1)
     lists(1, 1)
     for h in range(1, HOPS + 1):

from concourse.bass import DstId, RemoteDMATransfer
from concourse.mybir import AluOpType as Op, ActivationFunctionType as Act

N, HOPS, WORLD = 16, 4, 256
ONE = 262144.0
WIN = 2056
SCRATCH = {
    "fp": ("dram", [16, 128, 128], "int32"), "fv": ("dram", [16, 128, 128], "float32"),
    "tabp": ("sbuf", [128, WIN], "int32"), "tabv": ("sbuf", [128, WIN], "float32"),
    "own": ("sbuf", [128, 128], "int32"), "q0": ("sbuf", [128, 8], "int32"),
    "ri": ("sbuf", [128, 128], "int32"), "rj": ("sbuf", [128, 128], "int32"),
    "mx": ("sbuf", [128, 64], "float32"), "offs": ("sbuf", [128, 64], "uint16"),
    "gm": ("sbuf", [128, 1024], "float32"), "stt": ("sbuf", [128, 8, 32], "float32"),
    "stp": ("sbuf", [128, 8, 32], "float32"), "mk": ("sbuf", [128, 8, 18], "float32"),
    "zz": ("sbuf", [128, 128], "float32"), "zs": ("sbuf", [128, 128], "float32"), "keep": ("sbuf", [128, 64], "float32"),
    "ysb": ("sbuf", [128, 8], "float32"), "ybuf": ("sbuf", [128, 128], "float32"),
    "cmod": ("sbuf", [128, 128], "float32"), "cs": ("sbuf", [128, 32], "float32"), "mhc": ("sbuf", [128, 32], "float32"),
    "labs": ("sbuf", [128, 64], "float32"), "pidx": ("sbuf", [128, 1], "int32"), "pint": ("sbuf", [128, 2], "int32"),
    "pflt": ("sbuf", [128, 2], "float32"), "bias": ("sbuf", [128, 1], "float32"),
    "spread": ("sbuf", [128, 128], "float32"), "mmh": ("sbuf", [128, 32], "float32"),
    "selp": ("sbuf", [128, 32], "float32"), "selv": ("sbuf", [128, 16], "float32"),
    "cv0": ("psum", [128, 512], "float32"), "cv1": ("psum", [128, 512], "float32"),
    "li0": ("psum", [128, 512], "float32"), "li1": ("psum", [128, 512], "float32"), "lab": ("psum", [128, 512], "float32"),
}
SEMAPHORES = (["ldp", "ldv", "tpl", "tvl", "q0s", "q0r", "snd", "ya", "ys", "yd", "raw", "vc", "vn", "vi"]
              + ["ap%d" % r for r in range(N)] + ["av%d" % r for r in range(N)]
              + ["%s%d" % (s, k) for s in ("sc", "mx", "ri", "rj", "mk", "st", "of", "cs", "pl", "zz", "zs") for k in (0, 1)]
              + ["gc%d" % k for k in range(8)])
PLAN = {}


def bits(m):
    return bin(m).count("1")


def plan(T, topo):
    if PLAN:
        return PLAN
    chips = {}
    for c in range(WORLD):
        chips.setdefault((topo.host(c), topo.chip(c)), []).append(c)
    crews = list(chips.values())
    crew_of = {c: k for k in crews for c in k}
    cross = {c: [] for c in range(WORLD)}
    came = {c: 0 for c in range(WORLD)}
    enters = {}
    for r in range(N):
        home = T.cores[r]
        crew = crew_of[home]
        owners = [c for c in crew if all(topo.may_write(c, k[0]) for k in crews if k is not crew)]
        plain = [home] + [c for c in crew if c not in owners and c != home]
        at = crews.index(crew)
        for s in range(1, len(crews)):
            k = crews[(at + s) % len(crews)]
            who = min(plain if topo.same_plane(home, k[0]) else owners,
                      key=lambda c: (len(cross[c]), enters.get((k[0], topo.die(c)), 0)))
            cross[who].append(k)
            enters[(k[0], topo.die(who))] = enters.get((k[0], topo.die(who)), 0) + 1
            came[k[r // 2]] = bits(topo.mask(who, k[r // 2]))
    job, left = {}, []
    for r in range(N):
        for k, c in enumerate(crew_of[T.cores[r]]):
            job[c] = (r, k)
        left += [(r, k) for k in range(8, 16)]
    spare = [c for c in range(WORLD) if c not in job]
    spare.sort(key=lambda c: (sum(topo.may_write(c, d) for d in T.cores), c))
    asked = {}
    asks = {c: [] for c in range(WORLD)}
    for c in spare:
        r, k = min([x for x in left if topo.may_write(c, T.cores[x[0]])],
                   key=lambda x: (-sum(y[0] == x[0] for y in left), x))
        left.remove((r, k))
        job[c] = (r, k)
        who = min([d for d in crew_of[T.cores[r]] if topo.may_write(d, c)], key=lambda d: (len(asks[d]), len(cross[d])))
        asks[who].append((c, k))
        asked[c] = bits(topo.mask(who, c))
    PLAN.update(crew_of=crew_of, cross=cross, came=came, job=job, asks=asks, asked=asked)
    return PLAN


def rank_program(g, core, T, topo):
    pl = plan(T, topo)
    crew = pl["crew_of"][core]
    me = crew.index(core)
    others = [c for c in crew if c != core]
    rank = ([r for r in range(N) if T.cores[r] in crew] + [-1])[0]
    job, piece = pl["job"][core]
    home = T.cores[job]
    sent = [0]

    def send(src, dsts, sem):
        m = 0xFFFF
        for c, p in dsts:
            m &= topo.mask(core, c)
        ids = []
        for c, p in dsts:
            rid, pid = topo.addr(c, core)
            ids.append(DstId(rid=rid, pnc=pid))
        g.remote_dma_fused([RemoteDMATransfer(dst_ids=ids, dma_engine_mask=m, remote_sem=sem, srcs=[src],
                                              dsts=[p for c, p in dsts])], local_sem=T.sem.snd)
        sent[0] += bits(m)
    on_chip = bits(topo.mask(core, others[0]))
    slots = [r for r in (2 * me, 2 * me + 1) if r != rank]

    def here(q, r, what):
        if r == rank and core == home:
            q.wait_ge(T.sem["ld" + what], 16)
        else:
            q.wait_ge(T.sem["a%s%d" % (what, r)], pl["came"][core] if r in slots else on_chip)

    y, s = g.sync, g.scalar
    if core == home:
        y.dma_start(T.fp[rank], T.par[:]).then_inc(T.sem.ldp, 16)
        s.dma_start(T.own[:], T.par[:]).then_inc(T.sem.q0s, 16)
        s.dma_start(T.fv[rank], T.val[:]).then_inc(T.sem.ldv, 16)
    elif rank >= 0:
        here(s, rank, "p")
        s.dma_start(T.own[:], T.fp[rank]).then_inc(T.sem.q0s, 16)
    y.wait_ge(T.sem.vc, 4)
    for tab, full, what, done in ((T.tabp, T.fp, "p", T.sem.tpl), (T.tabv, T.fv, "v", T.sem.tvl)):
        for odd in (0, 1):
            for r in range(odd, N, 2):
                here(y, r, what)
            y.dma_start(tab[:, 4 + 1024 * odd:1028 + 1024 * odd], full[odd::2]).then_inc(done, 16)

    g.iota(T.pidx[:], [[0, 1]], 0, 1).then_inc(T.sem.raw, 1)
    for buf, pattern in ((T.cmod, [[0, 8], [1, 16]]), (T.cs, [[1, 32]]), (T.mhc, [[0, 4], [1, 8]]), (T.labs, [[0, 4], [1, 16]])):
        g.iota(buf[:], pattern, 0, 0, allow_small_or_imprecise_dtypes=True).then_inc(T.sem.raw, 1)

    def share(full, what):
        if core == home:
            here(g, rank, what)
            send(full[rank], [(c, full[rank]) for c in others], T.sem["a%s%d" % (what, rank)])

    def crossing(full, what):
        if pl["cross"][core]:
            here(g, rank, what)
            send(full[rank], [(k[rank // 2], full[rank]) for k in pl["cross"][core]], T.sem["a%s%d" % (what, rank)])

    def broadcast(full, what):
        for r in slots:
            here(g, r, what)
            send(full[r], [(c, full[r]) for c in others], T.sem["a%s%d" % (what, r)])
    share(T.fp, "p")
    crossing(T.fp, "p")
    if pl["asks"][core]:
        g.wait_ge(T.sem.q0s, 16)
        for c, k in pl["asks"][core]:
            send(T.own[:, 8 * k:8 * k + 8], [(c, T.q0[:])], T.sem.q0r)
    share(T.fv, "v")
    broadcast(T.fp, "p")
    crossing(T.fv, "v")
    broadcast(T.fv, "v")

    v, t = g.vector, g.tensor
    for tab in (T.tabp, T.tabv):
        v.memset(tab[:, 0:4], 0).then_inc(T.sem.vc, 1)
        v.memset(tab[:, WIN - 4:WIN], 0).then_inc(T.sem.vc, 1)
    n = [0]

    def con(ins):
        ins.then_inc(T.sem.vn, 1)
        n[0] += 1
    v.wait_ge(T.sem.raw, 5)
    con(v.tensor_scalar(T.pint[:, 0:1], T.pidx[:], 15, None, Op.bitwise_and))
    con(v.tensor_scalar(T.pint[:, 1:2], T.pidx[:], 4, None, Op.arith_shift_right))
    con(v.memset(T.stp[:], 0.0))
    con(v.memset(T.mk[:], 0.0))
    con(v.memset(T.keep[:], 1.0))
    v.wait_ge(T.sem.vn, n[0])
    con(v.tensor_copy(T.pflt[:], T.pint[:]))
    con(v.memset(T.keep[:, ::16], 0.0))
    con(v.tensor_copy(T.lab[:, 0:64], T.labs[:]))
    v.wait_ge(T.sem.vn, n[0])
    con(v.tensor_scalar(T.spread[:], T.cmod[:], T.pflt[:, 0:1], ONE / 16, Op.is_equal, Op.mult))
    con(v.tensor_scalar(T.selp[:], T.cs[:], T.pflt[:, 0:1], 1.0 / ONE, Op.is_equal, Op.mult))
    con(v.tensor_scalar(T.selv[:], T.cs[:, 0:16], T.pflt[:, 0:1], None, Op.is_equal))
    con(v.tensor_scalar(T.mmh[:], T.mhc[:], T.pflt[:, 1:2], None, Op.is_equal))
    con(v.tensor_scalar(T.bias[:], T.pflt[:, 1:2], -2048.0, 4.0 - 0.46875 - ONE / 16, Op.mult, Op.add))
    v.wait_ge(T.sem.vc, 4)
    v.wait_ge(T.sem.vn, n[0])
    if rank >= 0:
        v.wait_ge(T.sem.q0s, 16)
    else:
        v.wait_ge(T.sem.q0r, pl["asked"][core])
    for k in range(16, 32):
        v.tensor_scalar(T.stt[:, :, k], T.own[:, 8 * piece:8 * piece + 8] if rank >= 0 else T.q0[:], 1.0 / ONE, 1.0,
                        Op.mult, Op.add).then_inc(T.sem.vi, 1)
    v.wait_ge(T.sem.vi, 16)

    def masked(p, h):
        v.tensor_tensor(T.mx[:, 32 * p:32 * p + 32], T.stt[:, 4 * p:4 * p + 4, 16:24], T.mmh[:], Op.mult).then_inc(
            T.sem["mx%d" % p], 1)

    def low(p, h):
        a, b = 64 * p, 64 * p + 64
        v.tensor_scalar(T.ri[:, a:b], T.stt[:, 4 * p:4 * p + 4, 16:32], ONE, -ONE, Op.mult, Op.add).then_inc(T.sem["ri%d" % p], 1)
        v.wait_ge(T.sem["ri%d" % p], h)
        v.tensor_scalar(T.rj[:, a:b], T.ri[:, a:b], 15, None, Op.bitwise_and).then_inc(T.sem["rj%d" % p], 1)

    def choice(p, h):
        i, j = 4 * p, 4 * p + 4
        v.wait_ge(T.sem["rj%d" % p], h)
        v.tensor_tensor(T.mk[:, i:j, 1:17], T.rj[:, 64 * p:64 * p + 64], T.lab[:, 0:64], Op.is_equal).then_inc(
            T.sem["mk%d" % p], 1)
        if h < HOPS:
            v.wait_ge(T.sem["mk%d" % p], h)
            v.tensor_tensor(T.stp[:, i:j, 0:17], T.mk[:, i:j, 0:17], T.mk[:, i:j, 1:18], Op.subtract).then_inc(
                T.sem["st%d" % p], 1)

    def columns(p, h):
        v.wait_ge(T.sem["pl%d" % p], h)
        v.tensor_scalar(T.offs[:, 32 * p:32 * p + 32], T["li%d" % p][:, 0:32], T.bias[:, 0:1], 2052.0, Op.add, Op.min).then_inc(
            T.sem["of%d" % p], 1)

    def window(h):
        return (T.tabp if h < HOPS else T.tabv)[:, 0:WIN]

    def gather(p, h):
        v.wait_ge(T.sem["of%d" % p], h)
        for k in (4 * p, 4 * p + 1):
            v.tensor_copy(T.gm[:, 128 * k:128 * k + 128], window(h).indirect(T.offs[:, 8 * k:8 * k + 8])).then_inc(
                T.sem["gc%d" % k], 1)

    def pick(p, h):
        v.wait_ge(T.sem["cs%d" % p], 4 * h)
        v.wait_ge(T.sem["st%d" % p], h)
        for k in range(4):
            v.tensor_tensor_scan(T.stt[:, 4 * p + k, :], T.stp[:, 4 * p + k, :], T["cv%d" % p][:, 32 * k:32 * k + 32], 0.0,
                                 Op.add, Op.max).then_inc(T.sem["sc%d" % p], 1)
        v.wait_ge(T.sem["sc%d" % p], 4 * h)
        masked(p, h + 1)
        low(p, h + 1)

    for p in (0, 1):
        masked(p, 1)
        low(p, 1)
    for p in (0, 1):
        columns(p, 1)
        choice(p, 1)
    for q in (v, s):
        q.wait_ge(T.sem.tpl, 32)
    gather(0, 1)
    for h in range(1, HOPS + 1):
        if h > 1:
            if h == HOPS:
                v.wait_ge(T.sem.tvl, 32)
            gather(0, h)
            choice(0, h)
            pick(1, h - 1)
            columns(1, h)
        gather(1, h)
        if h > 1:
            choice(1, h)
        if h < HOPS:
            pick(0, h)
            columns(0, h + 1)
    out, base = (T.ybuf, 8 * piece) if core == home else (T.ysb, 0)
    for p in (0, 1):
        a, b = 64 * p, 64 * p + 64
        v.wait_ge(T.sem["cs%d" % p], 4 * HOPS)
        v.wait_ge(T.sem["mk%d" % p], HOPS)
        v.tensor_tensor(T.zz[:, a:b], T["cv%d" % p][:, 0:64], T.mk[:, 4 * p:4 * p + 4, 1:17], Op.mult).then_inc(T.sem["zz%d" % p], 1)
        v.wait_ge(T.sem["zz%d" % p], 1)
        v.tensor_tensor_scan(T.zs[:, a:b], T.keep[:], T.zz[:, a:b], 0.0, Op.mult, Op.add).then_inc(T.sem["zs%d" % p], 1)
        v.wait_ge(T.sem["zs%d" % p], 1)
        v.tensor_copy(out[:, base + 4 * p:base + 4 * p + 4], T.zs[:, a + 15:b:16]).then_inc(T.sem.ys, 1)
    for h in range(1, HOPS + 1):
        if h == HOPS:
            s.wait_ge(T.sem.tvl, 32)
        for p in (0, 1):
            s.wait_ge(T.sem["of%d" % p], h)
            for k in (4 * p + 2, 4 * p + 3):
                s.activation(T.gm[:, 128 * k:128 * k + 128], window(h).indirect(T.offs[:, 8 * k:8 * k + 8]), Act.Copy).then_inc(
                    T.sem["gc%d" % k], 1)

    def lists(p, h):
        t.wait_ge(T.sem["mx%d" % p], h)
        t.matmul(T["li%d" % p][:, 0:32], T.spread[:], T.mx[:, 32 * p:32 * p + 32], True, True).then_inc(T.sem["pl%d" % p], 1)

    def total(p, h, ks):
        w, sel = (32, T.selp) if h < HOPS else (16, T.selv)
        for k in ks:
            t.wait_ge(T.sem["gc%d" % (4 * p + k)], h)
            t.matmul(T["cv%d" % p][:, w * k:w * k + w], T.gm[:, 512 * p + 128 * k:512 * p + 128 * k + 128], sel[:],
                     True, True).then_inc(T.sem["cs%d" % p], 1)
    t.wait_ge(T.sem.vn, n[0])
    lists(0, 1)
    lists(1, 1)
    for h in range(1, HOPS + 1):
        total(0, h, (0, 2))
        if h > 1:
            lists(1, h)
        total(0, h, (1, 3))
        total(1, h, (0, 2))
        if h < HOPS:
            lists(0, h + 1)
        total(1, h, (1, 3))

    if core != home:
        g.wait_ge(T.sem.ys, 2)
        send(T.ysb[:], [(home, T.ybuf[:, 8 * piece:8 * piece + 8])], T.sem.ya)
    else:
        y.wait_ge(T.sem.ys, 2)
        y.wait_ge(T.sem.ya, sum(bits(topo.mask(c, core)) for c, x in pl["job"].items() if x[0] == job and c != core))
        y.dma_start(T.y[:], T.ybuf[:]).then_inc(T.sem.yd, 16)
        y.wait_ge(T.sem.yd, 16)
    g.wait_ge(T.sem.snd, sent[0])
